import numpy as np
import ml_dtypes


def mxq(x, axis, fmt="e4m3"):
    dtype, down = {"e4m3": (ml_dtypes.float8_e4m3fn, 7), "e5m2": (ml_dtypes.float8_e5m2, 14)}[fmt]
    v = np.moveaxis(np.asarray(x, np.float32).astype(ml_dtypes.bfloat16).astype(np.float64), axis, -1)
    blocks = v.reshape(v.shape[:-1] + (-1, 32))
    amax = np.abs(blocks).max(-1, keepdims=True)
    byte = np.maximum(np.where(amax > 0, np.frexp(amax)[1] - 1 + 127, 0) - down, 1)
    scale = np.exp2(byte - 127.0)
    codes = (blocks / scale).astype(np.float32).astype(dtype).astype(np.float64)
    return np.moveaxis((codes * scale).reshape(v.shape), -1, axis)


WIDE = False


def mx_kscale(k):
    if not WIDE:
        return np.ones(k)
    levels = np.array([30, -30])
    if k % 512:
        return np.exp2(np.random.permutation(np.resize(levels, k // 32))).repeat(32)
    a = np.empty((k // 512, 16))
    for p in range(k // 512):
        a[p, :8] = np.random.permutation(np.resize(levels, 8))
        for g in range(8):
            far = levels[np.abs(levels - a[p, g]) >= 10]
            a[p, g + 8] = far[np.random.randint(len(far))]
    return np.exp2(a.ravel()).repeat(32)


def f64(x):
    return np.asarray(x).astype(np.float64)


def striped(idx):
    return np.tile(np.asarray(idx).reshape(-1, 16).T, (8, 1)).astype(np.uint16)


def unstriped(offs):
    return offs[:16].T.reshape(-1).astype(np.int64)


E2M1 = np.array([0.0, 0.5, 1.0, 1.5, 2.0, 3.0, 4.0, 6.0, -0.0, -0.5, -1.0, -1.5, -2.0, -3.0, -4.0, -6.0])


def pack_weight(w, fmt):
    k, n = w.shape
    w = f64(np.asarray(w, np.float32).astype(ml_dtypes.bfloat16)).reshape(k // 32, 32, n)
    amax = np.abs(w).max(1)
    if fmt in ("e4m3", "e5m2"):
        byte = np.frexp(amax)[1] - 1 + 127 - (7 if fmt == "e4m3" else 14)
    else:
        mant, ex = np.frexp(amax / 6.0)
        byte = np.where(mant > 0.5, ex, ex - 1) + 127
    byte = np.clip(np.where(amax > 0, byte, 1), 1, 254)
    scaled = (w * np.exp2(127.0 - byte)[:, None, :]).reshape(k, n).astype(np.float32)
    by_word = np.ascontiguousarray(scaled.reshape(k // 512, 128, 4, n).transpose(0, 1, 3, 2))
    if fmt in ("e4m3", "e5m2"):
        words = by_word.astype(ml_dtypes.float8_e4m3fn if fmt == "e4m3" else ml_dtypes.float8_e5m2).view(np.uint8)
    else:
        c = by_word.astype(ml_dtypes.float4_e2m1fn).view(np.uint8) & 0xF
        words = (c[..., 0::2] | (c[..., 1::2] << 4)).reshape(k // 512, 128, 2 * n)
    return np.ascontiguousarray(words), np.ascontiguousarray(byte.astype(np.uint8).reshape(k // 512, 16, n))


def unpack_weight(words, scales, fmt):
    g, _, n = scales.shape
    words = np.ascontiguousarray(words).reshape(g, 128, n, -1)
    if fmt in ("e4m3", "e5m2"):
        vals = words.view(ml_dtypes.float8_e4m3fn if fmt == "e4m3" else ml_dtypes.float8_e5m2).astype(np.float64)
    else:
        nib = np.empty((g, 128, n, 4), np.uint8)
        nib[..., 0::2] = words & 0xF
        nib[..., 1::2] = words >> 4
        vals = E2M1[nib]
    vals = vals * np.repeat(np.exp2(scales.astype(np.float64) - 127.0), 8, axis=1)[..., None]
    return vals.transpose(0, 1, 3, 2).reshape(g * 512, n)


def sigmoid(v):
    return 1.0 / (1.0 + np.exp(-v))


def sgn(shape):
    return np.random.uniform(0.5, 2.0, shape) * np.where(np.random.standard_normal(shape) < 0, -1.0, 1.0)


K, T, J, R, V, N, U, E = 512, 1024, 256, 512, 1024, 256, 128, 512


def setup_inputs():
    n = np.random.standard_normal
    idx = np.random.permutation(V)[:R]
    idx2 = np.random.permutation(T)[:J]
    idx3 = np.random.permutation(J)[:U]
    idx4 = np.random.permutation(J)[:U]
    idx5 = np.random.permutation(E)[:U]
    idx6 = np.random.permutation(E)[:J]
    fk = mx_kscale(K)
    fr = mx_kscale(R)
    tr = np.ones(V)
    tr[idx] = fr
    xtp = pack_weight(n((K, T)) / fk[:, None], "e2m1")
    wtp = pack_weight(n((K, V)) * 1 / np.sqrt(K) * fk[:, None] * tr, "e4m3")
    w2p = pack_weight(n((K, R)) * 1 / np.sqrt(K) * fk[:, None] * fr, "e5m2")
    wbp = pack_weight(n((R, N)) * 1 / np.sqrt(R) / fr[:, None], "e2m1")
    wcp = pack_weight(n((R, N)) * 1 / np.sqrt(R) / fr[:, None], "e5m2")
    return {
        "xt_words": xtp[0],
        "xt_scales": xtp[1],
        "wt_words": wtp[0],
        "wt_scales": wtp[1],
        "w2_words": w2p[0],
        "w2_scales": w2p[1],
        "wb_words": wbp[0],
        "wb_scales": wbp[1],
        "wc_words": wcp[0],
        "wc_scales": wcp[1],
        "so": (np.random.uniform(0.5, 1.6, (N, 1))).astype(np.float32),
        "sp": (sgn((N, 1))).astype(np.float32),
        "bo": (np.random.uniform(-2.0, 2.0, (N, 1))).astype(np.float32),
        "offs": striped(idx),
        "offs2": striped(idx2),
        "offs3": striped(idx3),
        "offs4": striped(idx4),
        "offs5": striped(idx5),
        "offs6": striped(idx6),
    }


def reference(xt_words, xt_scales, wt_words, wt_scales, w2_words, w2_scales, wb_words, wb_scales, wc_words, wc_scales, so, sp, bo, offs, offs2, offs3, offs4, offs5, offs6):
    idx = unstriped(offs)
    idx2 = unstriped(offs2)
    idx3 = unstriped(offs3)
    idx4 = unstriped(offs4)
    idx5 = unstriped(offs5)
    idx6 = unstriped(offs6)
    xtu = unpack_weight(xt_words, xt_scales, "e2m1")
    wtu = unpack_weight(wt_words, wt_scales, "e4m3")
    w2u = unpack_weight(w2_words, w2_scales, "e5m2")
    wbu = unpack_weight(wb_words, wb_scales, "e2m1")
    wcu = unpack_weight(wc_words, wc_scales, "e5m2")
    wtidxg = wtu[:, idx]
    xtidx2g = xtu[:, idx2]
    a = wtidxg.T @ xtidx2g
    b = w2u.T @ xtidx2g
    hid = np.abs(a - b)
    hidq = mxq(hid, 0, "e5m2")
    p = wbu.T @ hidq
    q = wcu.T @ hidq
    m0 = p[:, idx3] * f64(so) * sigmoid(p[:, idx4] * f64(sp) + f64(bo))
    pw = np.zeros((N, E))
    pw[:, idx5] = m0
    pv = np.zeros((N, E))
    pv[:, idx6] = q
    y = pw + pv
    return y

@@ -1,0 +1,210 @@
+from contextlib import ExitStack
+
+import concourse.mybir as mybir
+
+K, T, J, R, V, N, U, E = 512, 1024, 256, 512, 1024, 256, 128, 512
+FLOPS = 2 * (2 * K * R * J + 2 * R * N * J)
+
+F32 = mybir.dt.float32
+BF16 = mybir.dt.bfloat16
+I32 = mybir.dt.int32
+U32 = mybir.dt.uint32
+U16 = mybir.dt.uint16
+U8 = mybir.dt.uint8
+E4M3 = mybir.dt.float8_e4m3fn_x4
+E5M2 = mybir.dt.float8_e5m2_x4
+E2M1 = mybir.dt.float4_e2m1fn_x4
+ALU = mybir.AluOpType
+ACT = mybir.ActivationFunctionType
+
+P = 128
+PACK = 4
+QUADS = 4
+HALF = J // 2
+CHUNK = HALF // 2
+BLOCKS = N // P
+
+
+def tile_list_outcomegatedpages_storeleads_kernel(
+    tc, xt_words, xt_scales, wt_words, wt_scales, w2_words, w2_scales, wb_words, wb_scales,
+    wc_words, wc_scales, so, sp, bo, offs, offs2, offs3, offs4, offs5, offs6, out,
+):
+    nc = tc.nc
+    with ExitStack() as ctx:
+        sb = ctx.enter_context(tc.tile_pool(name="sb", bufs=1))
+        ps = ctx.enter_context(tc.psum_pool(name="ps", bufs=1))
+
+        def tile(name, shape, dtype):
+            return sb.tile(shape, dtype, name=name, align_bytes=64)
+
+        def words(ap):
+            return ap.rearrange("p c t -> p (c t)").bitcast(I32)
+
+        def load_plane(queue, plane, scales):
+            for q in range(QUADS):
+                queue.dma_start(plane[32 * q : 32 * q + 4, :].bitcast(I32), scales[0, 4 * q : 4 * q + 4, :].bitcast(I32))
+
+        def load_staged(queue, staged, scales):
+            queue.dma_start(staged.bitcast(I32), scales[0].rearrange("(q r) c -> r q c", r=4).bitcast(I32))
+
+        def spread(plane, staged):
+            for q in range(QUADS):
+                nc.vector.tensor_copy(plane[32 * q : 32 * q + 4, :].bitcast(I32), staged[:, q, :].bitcast(I32))
+
+        def dealt(ap):
+            return ap.rearrange("p (t m) -> p m t", t=PACK)
+
+        list_wt = tile("list_wt", [P, R // 16], U16)
+        list_xt = tile("list_xt", [P, J // 16], U16)
+        list_val = tile("list_val", [P, U // 16], U16)
+        list_gate = tile("list_gate", [P, U // 16], U16)
+        list_m = tile("list_m", [P, U // 16], U16)
+        list_q = tile("list_q", [P, J // 16], U16)
+
+        xt_w = tile("xt_w", [P, T], U16)
+        xt_s = tile("xt_s", [P, T], U8)
+        wt_w = tile("wt_w", [P, V], U32)
+        wt_s = tile("wt_s", [P, V], U8)
+        w2_w = tile("w2_w", [P, R], U32)
+        w2_staged = tile("w2_staged", [4, QUADS, R], U8)
+        w2_s = tile("w2_s", [P, R], U8)
+        wb_w = tile("wb_w", [P, N], U16)
+        wc_w = tile("wc_w", [P, N], U32)
+        wb_s = tile("wb_s", [P, N], U8)
+        wc_s = tile("wc_s", [P, N], U8)
+        so_t = tile("so_t", [P, BLOCKS], F32)
+        sp_t = tile("sp_t", [P, BLOCKS], F32)
+        bo_t = tile("bo_t", [P, BLOCKS], F32)
+        page_m = [tile("page_m%d" % b, [P, E], F32) for b in range(BLOCKS)]
+        page_q = [tile("page_q%d" % b, [P, E], F32) for b in range(BLOCKS)]
+
+        for plane in (xt_s, wt_s):
+            nc.gpsimd.memset(plane[:].bitcast(I32), 0)
+        for plane in (w2_s, wc_s, wb_s):
+            nc.vector.memset(plane[:].bitcast(I32), 0)
+        for page in page_q + page_m:
+            nc.vector.memset(page[:], 0.0)
+
+        nc.sync.dma_start(list_xt[:], offs2)
+        nc.sync.dma_start(xt_w[:].bitcast(I32), xt_words[0].bitcast(I32))
+        load_plane(nc.scalar, xt_s, xt_scales)
+        load_staged(nc.sync, w2_staged[:], w2_scales)
+        nc.sync.dma_start(w2_w[:].bitcast(I32), words(w2_words[0]))
+        nc.sync.dma_start(list_wt[:], offs)
+        load_plane(nc.sync, wt_s, wt_scales)
+        nc.sync.dma_start(wt_w[:].bitcast(I32), words(wt_words[0]))
+        nc.sync.dma_start(wc_w[:].bitcast(I32), words(wc_words[0]))
+        nc.sync.dma_start(wb_w[:].bitcast(I32), wb_words[0].bitcast(I32))
+        load_plane(nc.sync, wc_s, wc_scales)
+        load_plane(nc.sync, wb_s, wb_scales)
+        nc.sync.dma_start(list_q[:], offs6)
+        nc.sync.dma_start(list_gate[:], offs4)
+        nc.sync.dma_start(list_val[:], offs3)
+        nc.sync.dma_start(list_m[:], offs5)
+        with nc.allow_non_contiguous_dma(reason="one value for each partition and block of rows"):
+            for column_tile, vector in ((sp_t, sp), (bo_t, bo), (so_t, so)):
+                nc.gpsimd.dma_start(column_tile[:], vector.rearrange("(b p) o -> p (b o)", p=P))
+
+        xg_s = tile("xg_s", [P, J], U8)
+        xg_w = tile("xg_w", [P, J], U16)
+        nc.vector.tensor_copy(xg_s[:], xt_s[:].indirect(list_xt[:]))
+        nc.vector.tensor_copy(xg_w[:], xt_w[:].indirect(list_xt[:]))
+
+        w2d_s = tile("w2d_s", [P, R], U8)
+        w2d_w = tile("w2d_w", [P, R], U32)
+        spread(w2_s, w2_staged)
+        nc.vector.tensor_copy(dealt(w2d_s[:]), w2_s[:].rearrange("p (m t) -> p m t", t=PACK))
+        nc.scalar.copy(dealt(w2d_w[:]), w2_w[:].rearrange("p (m t) -> p m t", t=PACK))
+
+        def first_stage(bank, h, lhs_w, lhs_s, fmt):
+            cols = slice(h * HALF, (h + 1) * HALF)
+            for t in range(PACK):
+                rows = slice(t * P, (t + 1) * P)
+                nc.tensor.matmul_mx(
+                    bank[:, t, :], lhsT=lhs_w[:, rows].bitcast(fmt), lhsT_scale=lhs_s[:, rows],
+                    rhs=xg_w[:, cols].bitcast(E2M1), rhs_scale=xg_s[:, cols], start=True, stop=True,
+                )
+
+        b_sb = []
+        for h in range(2):
+            bank = ps.tile([P, PACK, HALF], F32, name="bank_b%d" % h)
+            first_stage(bank, h, w2d_w, w2d_s, E5M2)
+            b_half = tile("b_sb%d" % h, [P, HALF, PACK], F32)
+            nc.scalar.copy(b_half[:], bank[:].rearrange("p t j -> p j t"))
+            b_sb.append(b_half)
+
+        wg_s = tile("wg_s", [P, R], U8)
+        wg_w = tile("wg_w", [P, R], U32)
+        nc.vector.tensor_copy(dealt(wg_s[:]), wt_s[:].indirect(list_wt[:]))
+        nc.vector.tensor_copy(dealt(wg_w[:]), wt_w[:].indirect(list_wt[:]))
+
+        hid = tile("hid", [P, J * PACK], BF16)
+        hq_w = tile("hq_w", [P, J], U32)
+        hq_s = tile("hq_s", [P, J], U8)
+        for h in range(2):
+            bank = ps.tile([P, PACK, HALF], F32, name="bank_a%d" % h)
+            first_stage(bank, h, wg_w, wg_s, E4M3)
+            for c in range(2):
+                js = slice(c * CHUNK, (c + 1) * CHUNK)
+                diff = tile("diff%d%d" % (h, c), [P, CHUNK, PACK], F32)
+                nc.vector.tensor_tensor(diff[:], bank[:, :, js].rearrange("p t j -> p j t"), b_sb[h][:, js, :], ALU.subtract)
+                first = (h * HALF + c * CHUNK) * PACK
+                nc.scalar.activation(hid[:, first : first + CHUNK * PACK], diff[:].rearrange("p j t -> p (j t)"), ACT.Abs)
+        for h in range(2):
+            cols = slice(h * HALF, (h + 1) * HALF)
+            nc.vector.quantize_mx(hq_w[:, cols].bitcast(E5M2), hq_s[:, cols], hid[:, h * HALF * PACK : (h + 1) * HALF * PACK])
+
+        bank_p = [ps.tile([P, 2, HALF], F32, name="bank_p%d" % b) for b in range(BLOCKS)]
+        bank_q = [ps.tile([P, BLOCKS, HALF], F32, name="bank_q%d" % h) for h in range(2)]
+
+        def second_stage(dst, h, b, lhs_w, lhs_s, fmt):
+            cols = slice(h * HALF, (h + 1) * HALF)
+            nc.tensor.matmul_mx(
+                dst, lhsT=lhs_w[:, b * P : (b + 1) * P].bitcast(fmt),
+                lhsT_scale=lhs_s[:, b * P : (b + 1) * P],
+                rhs=hq_w[:, cols].bitcast(E5M2), rhs_scale=hq_s[:, cols], start=True, stop=True,
+            )
+
+        for b in range(BLOCKS):
+            second_stage(bank_q[0][:, b, :], 0, b, wc_w, wc_s, E5M2)
+        for b in range(BLOCKS):
+            second_stage(bank_p[b][:, 0, :], 0, b, wb_w, wb_s, E2M1)
+        for b in range(BLOCKS):
+            second_stage(bank_p[b][:, 1, :], 1, b, wb_w, wb_s, E2M1)
+        for b in range(BLOCKS):
+            second_stage(bank_q[1][:, b, :], 1, b, wc_w, wc_s, E5M2)
+
+        p_sb = [tile("p_sb%d" % b, [P, J], F32) for b in range(BLOCKS)]
+        q_sb = [tile("q_sb%d" % h, [P, BLOCKS, HALF], F32) for h in range(2)]
+        gate = [tile("gate%d" % b, [P, U], F32) for b in range(BLOCKS)]
+        value = [tile("value%d" % b, [P, U], F32) for b in range(BLOCKS)]
+        result = [tile("result%d" % b, [P, E], F32) for b in range(BLOCKS)]
+
+        def q_window(b, h):
+            return page_q[b][:].indirect(list_q[:, h * HALF // 16 : (h + 1) * HALF // 16])
+
+        def look(b):
+            nc.scalar.activation(gate[b][:], p_sb[b][:].indirect(list_gate[:]), ACT.Sigmoid, bias=bo_t[:, b : b + 1], scale=sp_t[:, b : b + 1])
+            nc.scalar.activation(value[b][:], p_sb[b][:].indirect(list_val[:]), ACT.Copy, scale=so_t[:, b : b + 1])
+
+        def put_m(b):
+            nc.vector.tensor_tensor(page_m[b][:].indirect(list_m[:]), value[b][:], gate[b][:], ALU.mult)
+
+        def finish(b, cols):
+            nc.vector.tensor_tensor(result[b][:, cols], page_m[b][:, cols], page_q[b][:, cols], ALU.add)
+            nc.sync.dma_start(out[b * P : (b + 1) * P, cols], result[b][:, cols])
+
+        nc.scalar.copy(q_sb[0][:], bank_q[0][:])
+        nc.scalar.activation(q_window(0, 0), q_sb[0][:, 0, :], ACT.Copy)
+        for b in range(BLOCKS):
+            nc.vector.tensor_copy(p_sb[b][:], bank_p[b][:].rearrange("p h j -> p (h j)"))
+        nc.vector.tensor_copy(q_sb[1][:], bank_q[1][:])
+        nc.vector.tensor_copy(q_window(1, 0), q_sb[0][:, 1, :])
+        for b in range(BLOCKS):
+            look(b)
+            put_m(b)
+        for b in range(BLOCKS):
+            nc.scalar.activation(q_window(b, 1), q_sb[1][:, b, :], ACT.Copy)
+        finish(0, slice(0, E))
+        finish(1, slice(0, E // 2))
+        finish(1, slice(E // 2, E))

@@ -34,22 +34,15 @@ def tile_list_outcomegatedpages_storeleads_kernel(
         sb = ctx.enter_context(tc.tile_pool(name="sb", bufs=1))
         ps = ctx.enter_context(tc.psum_pool(name="ps", bufs=1))
 
-        def tile(name, shape, dtype):
-            return sb.tile(shape, dtype, name=name, align_bytes=64)
+        def tile(name, shape, dtype, tag=None):
+            return sb.tile(shape, dtype, name=name, tag=tag or name, align_bytes=64)
 
         def words(ap):
             return ap.rearrange("p c t -> p (c t)").bitcast(I32)
 
-        def load_plane(queue, plane, scales):
-            for q in range(QUADS):
+        def load_plane(queue, plane, scales, quadrants=range(QUADS)):
+            for q in quadrants:
                 queue.dma_start(plane[32 * q : 32 * q + 4, :].bitcast(I32), scales[0, 4 * q : 4 * q + 4, :].bitcast(I32))
-
-        def load_staged(queue, staged, scales):
-            queue.dma_start(staged.bitcast(I32), scales[0].rearrange("(q r) c -> r q c", r=4).bitcast(I32))
-
-        def spread(plane, staged):
-            for q in range(QUADS):
-                nc.vector.tensor_copy(plane[32 * q : 32 * q + 4, :].bitcast(I32), staged[:, q, :].bitcast(I32))
 
         def dealt(ap):
             return ap.rearrange("p (t m) -> p m t", t=PACK)
@@ -66,7 +59,6 @@ def tile_list_outcomegatedpages_storeleads_kernel(
         wt_w = tile("wt_w", [P, V], U32)
         wt_s = tile("wt_s", [P, V], U8)
         w2_w = tile("w2_w", [P, R], U32)
-        w2_staged = tile("w2_staged", [4, QUADS, R], U8)
         w2_s = tile("w2_s", [P, R], U8)
         wb_w = tile("wb_w", [P, N], U16)
         wc_w = tile("wc_w", [P, N], U32)
@@ -78,24 +70,28 @@ def tile_list_outcomegatedpages_storeleads_kernel(
         page_m = [tile("page_m%d" % b, [P, E], F32) for b in range(BLOCKS)]
         page_q = [tile("page_q%d" % b, [P, E], F32) for b in range(BLOCKS)]
 
-        for plane in (xt_s, wt_s):
+        for plane in (xt_s, wt_s, w2_s):
             nc.gpsimd.memset(plane[:].bitcast(I32), 0)
-        for plane in (w2_s, wc_s, wb_s):
+        for plane in (wc_s, wb_s):
             nc.vector.memset(plane[:].bitcast(I32), 0)
         for page in page_q + page_m:
             nc.vector.memset(page[:], 0.0)
+        warm_in = tile("warm_in", [P, 1], F32)
+        warm_out = tile("warm_out", [P, 1], F32)
+        nc.vector.memset(warm_in[:], 0.0)
 
+        load_plane(nc.gpsimd, wt_s, wt_scales, [QUADS - 1])
         nc.sync.dma_start(list_xt[:], offs2)
         nc.sync.dma_start(xt_w[:].bitcast(I32), xt_words[0].bitcast(I32))
-        load_plane(nc.scalar, xt_s, xt_scales)
-        load_staged(nc.sync, w2_staged[:], w2_scales)
-        nc.sync.dma_start(w2_w[:].bitcast(I32), words(w2_words[0]))
         nc.sync.dma_start(list_wt[:], offs)
-        load_plane(nc.sync, wt_s, wt_scales)
+        load_plane(nc.sync, xt_s, xt_scales)
         nc.sync.dma_start(wt_w[:].bitcast(I32), words(wt_words[0]))
+        nc.sync.dma_start(w2_w[:].bitcast(I32), words(w2_words[0]))
+        load_plane(nc.sync, w2_s, w2_scales)
+        load_plane(nc.sync, wt_s, wt_scales, range(QUADS - 1))
         nc.sync.dma_start(wc_w[:].bitcast(I32), words(wc_words[0]))
-        nc.sync.dma_start(wb_w[:].bitcast(I32), wb_words[0].bitcast(I32))
         load_plane(nc.sync, wc_s, wc_scales)
+        nc.sync.dma_start(wb_w[:].bitcast(I32), wb_words[0].bitcast(I32))
         load_plane(nc.sync, wb_s, wb_scales)
         nc.sync.dma_start(list_q[:], offs6)
         nc.sync.dma_start(list_gate[:], offs4)
@@ -105,14 +101,14 @@ def tile_list_outcomegatedpages_storeleads_kernel(
             for column_tile, vector in ((sp_t, sp), (bo_t, bo), (so_t, so)):
                 nc.gpsimd.dma_start(column_tile[:], vector.rearrange("(b p) o -> p (b o)", p=P))
 
+        nc.scalar.activation(warm_out[:], warm_in[:], ACT.Sigmoid)
         xg_s = tile("xg_s", [P, J], U8)
         xg_w = tile("xg_w", [P, J], U16)
-        nc.vector.tensor_copy(xg_s[:], xt_s[:].indirect(list_xt[:]))
         nc.vector.tensor_copy(xg_w[:], xt_w[:].indirect(list_xt[:]))
+        nc.vector.tensor_copy(xg_s[:], xt_s[:].indirect(list_xt[:]))
 
         w2d_s = tile("w2d_s", [P, R], U8)
         w2d_w = tile("w2d_w", [P, R], U32)
-        spread(w2_s, w2_staged)
         nc.vector.tensor_copy(dealt(w2d_s[:]), w2_s[:].rearrange("p (m t) -> p m t", t=PACK))
         nc.scalar.copy(dealt(w2d_w[:]), w2_w[:].rearrange("p (m t) -> p m t", t=PACK))
 
@@ -135,8 +131,8 @@ def tile_list_outcomegatedpages_storeleads_kernel(
 
         wg_s = tile("wg_s", [P, R], U8)
         wg_w = tile("wg_w", [P, R], U32)
-        nc.vector.tensor_copy(dealt(wg_s[:]), wt_s[:].indirect(list_wt[:]))
         nc.vector.tensor_copy(dealt(wg_w[:]), wt_w[:].indirect(list_wt[:]))
+        nc.vector.tensor_copy(dealt(wg_s[:]), wt_s[:].indirect(list_wt[:]))
 
         hid = tile("hid", [P, J * PACK], BF16)
         hq_w = tile("hq_w", [P, J], U32)
@@ -175,7 +171,7 @@ def tile_list_outcomegatedpages_storeleads_kernel(
             second_stage(bank_q[1][:, b, :], 1, b, wc_w, wc_s, E5M2)
 
         p_sb = [tile("p_sb%d" % b, [P, J], F32) for b in range(BLOCKS)]
-        q_sb = [tile("q_sb%d" % h, [P, BLOCKS, HALF], F32) for h in range(2)]
+        q_sb = [tile("q_sb0", [P, BLOCKS, HALF], F32)]
         gate = [tile("gate%d" % b, [P, U], F32) for b in range(BLOCKS)]
         value = [tile("value%d" % b, [P, U], F32) for b in range(BLOCKS)]
         result = [tile("result%d" % b, [P, E], F32) for b in range(BLOCKS)]
@@ -198,10 +194,12 @@ def tile_list_outcomegatedpages_storeleads_kernel(
         nc.scalar.activation(q_window(0, 0), q_sb[0][:, 0, :], ACT.Copy)
         for b in range(BLOCKS):
             nc.vector.tensor_copy(p_sb[b][:], bank_p[b][:].rearrange("p h j -> p (h j)"))
-        nc.vector.tensor_copy(q_sb[1][:], bank_q[1][:])
         nc.vector.tensor_copy(q_window(1, 0), q_sb[0][:, 1, :])
         for b in range(BLOCKS):
             look(b)
+        q_sb.append(tile("q_sb1", [P, BLOCKS, HALF], F32, tag="p_sb0"))
+        nc.vector.tensor_copy(q_sb[1][:], bank_q[1][:])
+        for b in range(BLOCKS):
             put_m(b)
         for b in range(BLOCKS):
             nc.scalar.activation(q_window(b, 1), q_sb[1][:, b, :], ACT.Copy)

from contextlib import ExitStack

import concourse.mybir as mybir

K, T, J, R, V, N, U, E = 512, 1024, 256, 512, 1024, 256, 128, 512
FLOPS = 2 * (2 * K * R * J + 2 * R * N * J)

F32 = mybir.dt.float32
BF16 = mybir.dt.bfloat16
I32 = mybir.dt.int32
U32 = mybir.dt.uint32
U16 = mybir.dt.uint16
U8 = mybir.dt.uint8
E4M3 = mybir.dt.float8_e4m3fn_x4
E5M2 = mybir.dt.float8_e5m2_x4
E2M1 = mybir.dt.float4_e2m1fn_x4
ALU = mybir.AluOpType
ACT = mybir.ActivationFunctionType

P = 128
PACK = 4
QUADS = 4
HALF = J // 2
CHUNK = HALF // 2
BLOCKS = N // P


def tile_list_outcomegatedpages_storeleads_kernel(
    tc, xt_words, xt_scales, wt_words, wt_scales, w2_words, w2_scales, wb_words, wb_scales,
    wc_words, wc_scales, so, sp, bo, offs, offs2, offs3, offs4, offs5, offs6, out,
):
    nc = tc.nc
    with ExitStack() as ctx:
        sb = ctx.enter_context(tc.tile_pool(name="sb", bufs=1))
        ps = ctx.enter_context(tc.psum_pool(name="ps", bufs=1))

        def tile(name, shape, dtype, tag=None):
            return sb.tile(shape, dtype, name=name, tag=tag or name, align_bytes=64)

        def words(ap):
            return ap.rearrange("p c t -> p (c t)").bitcast(I32)

        def load_plane(queue, plane, scales, quadrants=range(QUADS)):
            for q in quadrants:
                queue.dma_start(plane[32 * q : 32 * q + 4, :].bitcast(I32), scales[0, 4 * q : 4 * q + 4, :].bitcast(I32))

        def dealt(ap):
            return ap.rearrange("p (t m) -> p m t", t=PACK)

        list_wt = tile("list_wt", [P, R // 16], U16)
        list_xt = tile("list_xt", [P, J // 16], U16)
        list_val = tile("list_val", [P, U // 16], U16)
        list_gate = tile("list_gate", [P, U // 16], U16)
        list_m = tile("list_m", [P, U // 16], U16)
        list_q = tile("list_q", [P, J // 16], U16)

        xt_w = tile("xt_w", [P, T], U16)
        xt_s = tile("xt_s", [P, T], U8)
        wt_w = tile("wt_w", [P, V], U32)
        wt_s = tile("wt_s", [P, V], U8)
        w2_w = tile("w2_w", [P, R], U32)
        w2_s = tile("w2_s", [P, R], U8)
        wb_w = tile("wb_w", [P, N], U16)
        wc_w = tile("wc_w", [P, N], U32)
        wb_s = tile("wb_s", [P, N], U8)
        wc_s = tile("wc_s", [P, N], U8)
        so_t = tile("so_t", [P, BLOCKS], F32)
        sp_t = tile("sp_t", [P, BLOCKS], F32)
        bo_t = tile("bo_t", [P, BLOCKS], F32)
        page_m = [tile("page_m%d" % b, [P, E], F32) for b in range(BLOCKS)]
        page_q = [tile("page_q%d" % b, [P, E], F32) for b in range(BLOCKS)]

        for plane in (xt_s, wt_s, w2_s):
            nc.gpsimd.memset(plane[:].bitcast(I32), 0)
        for plane in (wc_s, wb_s):
            nc.vector.memset(plane[:].bitcast(I32), 0)
        for page in page_q + page_m:
            nc.vector.memset(page[:], 0.0)
        warm_in = tile("warm_in", [P, 1], F32)
        warm_out = tile("warm_out", [P, 1], F32)
        nc.vector.memset(warm_in[:], 0.0)

        load_plane(nc.gpsimd, wt_s, wt_scales, [QUADS - 1])
        nc.sync.dma_start(list_xt[:], offs2)
        nc.sync.dma_start(xt_w[:].bitcast(I32), xt_words[0].bitcast(I32))
        nc.sync.dma_start(list_wt[:], offs)
        load_plane(nc.sync, xt_s, xt_scales)
        nc.sync.dma_start(wt_w[:].bitcast(I32), words(wt_words[0]))
        nc.sync.dma_start(w2_w[:].bitcast(I32), words(w2_words[0]))
        load_plane(nc.sync, w2_s, w2_scales)
        load_plane(nc.sync, wt_s, wt_scales, range(QUADS - 1))
        nc.sync.dma_start(wc_w[:].bitcast(I32), words(wc_words[0]))
        load_plane(nc.sync, wc_s, wc_scales)
        nc.sync.dma_start(wb_w[:].bitcast(I32), wb_words[0].bitcast(I32))
        load_plane(nc.sync, wb_s, wb_scales)
        nc.sync.dma_start(list_q[:], offs6)
        nc.sync.dma_start(list_gate[:], offs4)
        nc.sync.dma_start(list_val[:], offs3)
        nc.sync.dma_start(list_m[:], offs5)
        with nc.allow_non_contiguous_dma(reason="one value for each partition and block of rows"):
            for column_tile, vector in ((sp_t, sp), (bo_t, bo), (so_t, so)):
                nc.gpsimd.dma_start(column_tile[:], vector.rearrange("(b p) o -> p (b o)", p=P))

        nc.scalar.activation(warm_out[:], warm_in[:], ACT.Sigmoid)
        xg_s = tile("xg_s", [P, J], U8)
        xg_w = tile("xg_w", [P, J], U16)
        nc.vector.tensor_copy(xg_w[:], xt_w[:].indirect(list_xt[:]))
        nc.vector.tensor_copy(xg_s[:], xt_s[:].indirect(list_xt[:]))

        w2d_s = tile("w2d_s", [P, R], U8)
        w2d_w = tile("w2d_w", [P, R], U32)
        nc.vector.tensor_copy(dealt(w2d_s[:]), w2_s[:].rearrange("p (m t) -> p m t", t=PACK))
        nc.scalar.copy(dealt(w2d_w[:]), w2_w[:].rearrange("p (m t) -> p m t", t=PACK))

        def first_stage(bank, h, lhs_w, lhs_s, fmt):
            cols = slice(h * HALF, (h + 1) * HALF)
            for t in range(PACK):
                rows = slice(t * P, (t + 1) * P)
                nc.tensor.matmul_mx(
                    bank[:, t, :], lhsT=lhs_w[:, rows].bitcast(fmt), lhsT_scale=lhs_s[:, rows],
                    rhs=xg_w[:, cols].bitcast(E2M1), rhs_scale=xg_s[:, cols], start=True, stop=True,
                )

        b_sb = []
        for h in range(2):
            bank = ps.tile([P, PACK, HALF], F32, name="bank_b%d" % h)
            first_stage(bank, h, w2d_w, w2d_s, E5M2)
            b_half = tile("b_sb%d" % h, [P, HALF, PACK], F32)
            nc.scalar.copy(b_half[:], bank[:].rearrange("p t j -> p j t"))
            b_sb.append(b_half)

        wg_s = tile("wg_s", [P, R], U8)
        wg_w = tile("wg_w", [P, R], U32)
        nc.vector.tensor_copy(dealt(wg_w[:]), wt_w[:].indirect(list_wt[:]))
        nc.vector.tensor_copy(dealt(wg_s[:]), wt_s[:].indirect(list_wt[:]))

        hid = tile("hid", [P, J * PACK], BF16)
        hq_w = tile("hq_w", [P, J], U32)
        hq_s = tile("hq_s", [P, J], U8)
        for h in range(2):
            bank = ps.tile([P, PACK, HALF], F32, name="bank_a%d" % h)
            first_stage(bank, h, wg_w, wg_s, E4M3)
            for c in range(2):
                js = slice(c * CHUNK, (c + 1) * CHUNK)
                diff = tile("diff%d%d" % (h, c), [P, CHUNK, PACK], F32)
                nc.vector.tensor_tensor(diff[:], bank[:, :, js].rearrange("p t j -> p j t"), b_sb[h][:, js, :], ALU.subtract)
                first = (h * HALF + c * CHUNK) * PACK
                nc.scalar.activation(hid[:, first : first + CHUNK * PACK], diff[:].rearrange("p j t -> p (j t)"), ACT.Abs)
        for h in range(2):
            cols = slice(h * HALF, (h + 1) * HALF)
            nc.vector.quantize_mx(hq_w[:, cols].bitcast(E5M2), hq_s[:, cols], hid[:, h * HALF * PACK : (h + 1) * HALF * PACK])

        bank_p = [ps.tile([P, 2, HALF], F32, name="bank_p%d" % b) for b in range(BLOCKS)]
        bank_q = [ps.tile([P, BLOCKS, HALF], F32, name="bank_q%d" % h) for h in range(2)]

        def second_stage(dst, h, b, lhs_w, lhs_s, fmt):
            cols = slice(h * HALF, (h + 1) * HALF)
            nc.tensor.matmul_mx(
                dst, lhsT=lhs_w[:, b * P : (b + 1) * P].bitcast(fmt),
                lhsT_scale=lhs_s[:, b * P : (b + 1) * P],
                rhs=hq_w[:, cols].bitcast(E5M2), rhs_scale=hq_s[:, cols], start=True, stop=True,
            )

        for b in range(BLOCKS):
            second_stage(bank_q[0][:, b, :], 0, b, wc_w, wc_s, E5M2)
        for b in range(BLOCKS):
            second_stage(bank_p[b][:, 0, :], 0, b, wb_w, wb_s, E2M1)
        for b in range(BLOCKS):
            second_stage(bank_p[b][:, 1, :], 1, b, wb_w, wb_s, E2M1)
        for b in range(BLOCKS):
            second_stage(bank_q[1][:, b, :], 1, b, wc_w, wc_s, E5M2)

        p_sb = [tile("p_sb%d" % b, [P, J], F32) for b in range(BLOCKS)]
        q_sb = [tile("q_sb0", [P, BLOCKS, HALF], F32)]
        gate = [tile("gate%d" % b, [P, U], F32) for b in range(BLOCKS)]
        value = [tile("value%d" % b, [P, U], F32) for b in range(BLOCKS)]
        result = [tile("result%d" % b, [P, E], F32) for b in range(BLOCKS)]

        def q_window(b, h):
            return page_q[b][:].indirect(list_q[:, h * HALF // 16 : (h + 1) * HALF // 16])

        def look(b):
            nc.scalar.activation(gate[b][:], p_sb[b][:].indirect(list_gate[:]), ACT.Sigmoid, bias=bo_t[:, b : b + 1], scale=sp_t[:, b : b + 1])
            nc.scalar.activation(value[b][:], p_sb[b][:].indirect(list_val[:]), ACT.Copy, scale=so_t[:, b : b + 1])

        def put_m(b):
            nc.vector.tensor_tensor(page_m[b][:].indirect(list_m[:]), value[b][:], gate[b][:], ALU.mult)

        def finish(b, cols):
            nc.vector.tensor_tensor(result[b][:, cols], page_m[b][:, cols], page_q[b][:, cols], ALU.add)
            nc.sync.dma_start(out[b * P : (b + 1) * P, cols], result[b][:, cols])

        nc.scalar.copy(q_sb[0][:], bank_q[0][:])
        nc.scalar.activation(q_window(0, 0), q_sb[0][:, 0, :], ACT.Copy)
        for b in range(BLOCKS):
            nc.vector.tensor_copy(p_sb[b][:], bank_p[b][:].rearrange("p h j -> p (h j)"))
        nc.vector.tensor_copy(q_window(1, 0), q_sb[0][:, 1, :])
        for b in range(BLOCKS):
            look(b)
        q_sb.append(tile("q_sb1", [P, BLOCKS, HALF], F32, tag="p_sb0"))
        nc.vector.tensor_copy(q_sb[1][:], bank_q[1][:])
        for b in range(BLOCKS):
            put_m(b)
        for b in range(BLOCKS):
            nc.scalar.activation(q_window(b, 1), q_sb[1][:, b, :], ACT.Copy)
        finish(0, slice(0, E))
        finish(1, slice(0, E // 2))
        finish(1, slice(E // 2, E))
